import numpy as np
import ml_dtypes


def mxq(x, axis, fmt="e4m3"):
    dtype, down = {"e4m3": (ml_dtypes.float8_e4m3fn, 7), "e5m2": (ml_dtypes.float8_e5m2, 14)}[fmt]
    v = np.moveaxis(np.asarray(x, np.float32).astype(ml_dtypes.bfloat16).astype(np.float64), axis, -1)
    blocks = v.reshape(v.shape[:-1] + (-1, 32))
    amax = np.abs(blocks).max(-1, keepdims=True)
    byte = np.maximum(np.where(amax > 0, np.frexp(amax)[1] - 1 + 127, 0) - down, 1)
    scale = np.exp2(byte - 127.0)
    codes = (blocks / scale).astype(np.float32).astype(dtype).astype(np.float64)
    return np.moveaxis((codes * scale).reshape(v.shape), -1, axis)


WIDE = False


def mx_kscale(k):
    if not WIDE:
        return np.ones(k)
    levels = np.array([10, -10, 5, -5, 0])
    if k % 512:
        return np.exp2(np.random.permutation(np.resize(levels, k // 32))).repeat(32)
    a = np.empty((k // 512, 16))
    for p in range(k // 512):
        a[p, :8] = np.random.permutation(np.resize(levels, 8))
        for g in range(8):
            far = levels[np.abs(levels - a[p, g]) >= 10]
            a[p, g + 8] = far[np.random.randint(len(far))]
    return np.exp2(a.ravel()).repeat(32)


def f64(x):
    return np.asarray(x).astype(np.float64)


E2M1 = np.array([0.0, 0.5, 1.0, 1.5, 2.0, 3.0, 4.0, 6.0, -0.0, -0.5, -1.0, -1.5, -2.0, -3.0, -4.0, -6.0])


def pack_weight(w, fmt):
    k, n = w.shape
    w = f64(np.asarray(w, np.float32).astype(ml_dtypes.bfloat16)).reshape(k // 32, 32, n)
    amax = np.abs(w).max(1)
    if fmt == "e4m3":
        byte = np.frexp(amax)[1] - 1 + 127 - 7
    else:
        mant, ex = np.frexp(amax / 6.0)
        byte = np.where(mant > 0.5, ex, ex - 1) + 127
    byte = np.clip(np.where(amax > 0, byte, 1), 1, 254)
    scaled = (w * np.exp2(127.0 - byte)[:, None, :]).reshape(k, n).astype(np.float32)
    by_word = np.ascontiguousarray(scaled.reshape(k // 512, 128, 4, n).transpose(0, 1, 3, 2))
    if fmt == "e4m3":
        words = by_word.astype(ml_dtypes.float8_e4m3fn).view(np.uint8)
    else:
        c = by_word.astype(ml_dtypes.float4_e2m1fn).view(np.uint8) & 0xF
        words = (c[..., 0::2] | (c[..., 1::2] << 4)).reshape(k // 512, 128, 2 * n)
    return np.ascontiguousarray(words), np.ascontiguousarray(byte.astype(np.uint8).reshape(k // 512, 16, n))


def unpack_weight(words, scales, fmt):
    g, _, n = scales.shape
    words = np.ascontiguousarray(words).reshape(g, 128, n, -1)
    if fmt == "e4m3":
        vals = words.view(ml_dtypes.float8_e4m3fn).astype(np.float64)
    else:
        nib = np.empty((g, 128, n, 4), np.uint8)
        nib[..., 0::2] = words & 0xF
        nib[..., 1::2] = words >> 4
        vals = E2M1[nib]
    vals = vals * np.repeat(np.exp2(scales.astype(np.float64) - 127.0), 8, axis=1)[..., None]
    return vals.transpose(0, 1, 3, 2).reshape(g * 512, n)


K, M, T = 1024, 1024, 1024


def setup_inputs():
    n = np.random.standard_normal
    s = mx_kscale(K)[:, None]
    x = n((K, T)) * s
    x4 = pack_weight(x, "e2m1")
    rest = x - unpack_weight(*x4, "e2m1")
    p_w4 = pack_weight(n((K, M)) / np.sqrt(K) / s, "e2m1")
    return {
        "x4_words": x4[0],
        "x4_scales": x4[1],
        "xr": (rest).astype(np.float32),
        "w4_words": p_w4[0],
        "w4_scales": p_w4[1],
        "b": (0.3 * n(1024)).astype(np.float32),
    }


def reference(x4_words, x4_scales, xr, w4_words, w4_scales, b):
    x4_ = unpack_weight(x4_words, x4_scales, "e2m1")
    xr_ = mxq(f64(xr), 0, "e4m3")
    w4_ = unpack_weight(w4_words, w4_scales, "e2m1")
    y = x4_.T @ w4_ + xr_.T @ w4_
    return y + f64(b)[None, :]

@@ -1,0 +1,203 @@
+from contextlib import ExitStack
+
+import concourse.mybir as mybir
+
+F32 = mybir.dt.float32
+BF16 = mybir.dt.bfloat16
+I32 = mybir.dt.int32
+U32 = mybir.dt.uint32
+U8 = mybir.dt.uint8
+E4M3 = mybir.dt.float8_e4m3fn_x4
+E2M1 = mybir.dt.float4_e2m1fn_x4
+ADD = mybir.AluOpType.add
+
+P = 128
+K, N, T = 1024, 1024, 1024
+PASSES = K // 512
+HALF = 512
+Q = 256
+FLOPS = 2 * 2 * K * N * T
+
+
+def tile_mix_xres_tm_bias_kernel(tc, x4_words, x4_scales, xr, w4_words, w4_scales, b, out):
+    nc = tc.nc
+    with ExitStack() as ctx:
+        keep = ctx.enter_context(tc.tile_pool(name="keep", bufs=1))
+        psum = ctx.enter_context(tc.psum_pool(name="psum", bufs=8))
+        ctx.enter_context(tc.manual_schedule())
+
+        def sb(name, shape, dtype):
+            return keep.tile(shape, dtype, name=name, align_bytes=256)
+
+        ws = sb("ws", [P, PASSES * N], U8)
+        xs = sb("xs", [P, PASSES * T], U8)
+        w = [sb(f"w{a}", [P, 2 * N], U8) for a in range(PASSES)]
+        x_half = [sb(f"x{h}", [P, PASSES * T], U8) for h in range(2)]
+
+        nc.vector.memset(ws[:].bitcast(I32), 0)
+        nc.vector.memset(xs[:].bitcast(I32), 0)
+        warm = sb("warm", [P, 2], F32)
+        nc.vector.memset(warm[:, 0:1], 0.0)
+
+        def load_scales(eng, plane, scales, quad):
+            eng.dma_start(
+                out=plane[32 * quad : 32 * quad + 4, :].bitcast(I32).rearrange("p (a n) -> p a n", a=PASSES),
+                in_=scales.bitcast(I32)[:, 4 * quad : 4 * quad + 4, :].rearrange("a r n -> r a n"),
+            )
+
+        def load_x4(eng, h):
+            eng.dma_start(
+                out=x_half[h][:].bitcast(I32).rearrange("p (a t) -> p a t", a=PASSES),
+                in_=x4_words.bitcast(I32)[:, :, 256 * h : 256 * h + 256].rearrange("a p t -> p a t"),
+            )
+
+        nc.sync.dma_start(out=w[0][:].bitcast(I32), in_=w4_words[0].bitcast(I32))
+        load_x4(nc.scalar, 0)
+        for quad in range(4):
+            load_scales(nc.sync, ws, w4_scales, quad)
+            load_scales(nc.scalar, xs, x4_scales, quad)
+
+        xr_v = xr.rearrange("(a p j) t -> a p j t", a=PASSES, j=4)
+
+        def load_xr(name, a, t0, width):
+            raw = sb(name, [P, 4, width], F32)
+            nc.sync.dma_start(out=raw[:], in_=xr_v[a, :, :, t0 : t0 + width])
+            return raw
+
+        raw00 = load_xr("raw00", 0, 0, 512)
+        nc.sync.dma_start(out=w[1][:].bitcast(I32), in_=w4_words[1].bitcast(I32))
+        bz = sb("bz", [P, 32], F32)
+        for quad in range(4):
+            nc.sync.dma_start(out=bz[32 * quad : 32 * quad + 32, :], in_=b.rearrange("(j q) -> j q", q=32))
+        raw10 = load_xr("raw10", 1, 0, 256)
+        raw11 = load_xr("raw11", 1, 256, 256)
+        load_x4(nc.sync, 1)
+        raw02 = load_xr("raw02", 0, 512, 512)
+        raw12 = load_xr("raw12", 1, 512, 512)
+        raw_of = {
+            (0, 0): raw00[:, :, 0:256],
+            (0, 1): raw00[:, :, 256:512],
+            (1, 0): raw10[:],
+            (1, 1): raw11[:],
+            (0, 2): raw02[:, :, 0:256],
+            (0, 3): raw02[:, :, 256:512],
+            (1, 2): raw12[:, :, 0:256],
+            (1, 3): raw12[:, :, 256:512],
+        }
+        grouped = {key: sb(f"g{key[0]}{key[1]}", [P, Q * 4], BF16) for key in raw_of}
+        codes = {key: sb(f"c{key[0]}{key[1]}", [P, Q], U32) for key in raw_of}
+        planes = {key: sb(f"s{key[0]}{key[1]}", [P, Q], U8) for key in raw_of}
+
+        def cast(eng_copy, a, q):
+            eng_copy(
+                out=grouped[a, q][:].rearrange("p (c i j) -> p c j i", i=4, j=4),
+                in_=raw_of[a, q].rearrange("p j (c i) -> p c j i", i=4),
+            )
+
+        def quant(a, q):
+            nc.vector.quantize_mx(out=codes[a, q][:].bitcast(E4M3), scales=planes[a, q][:], in_=grouped[a, q][:])
+
+        def w_ops(a, n0, width):
+            return (
+                w[a][:, 2 * n0 : 2 * n0 + 2 * width].bitcast(E2M1),
+                ws[:, N * a + n0 : N * a + n0 + width],
+            )
+
+        def x4_pass(acc, t, n0, width, a):
+            rhs, rhs_scale = w_ops(a, n0, width)
+            h, i = divmod(t, 4)
+            nc.tensor.matmul_mx(
+                out=acc[:],
+                lhsT=x_half[h][:, 1024 * a + 256 * i : 1024 * a + 256 * i + 256].bitcast(E2M1),
+                lhsT_scale=xs[:, T * a + P * t : T * a + P * t + P],
+                rhs=rhs,
+                rhs_scale=rhs_scale,
+                start=(a == 0),
+                stop=False,
+            )
+
+        def xr_pass(acc, t, n0, width, a):
+            rhs, rhs_scale = w_ops(a, n0, width)
+            q, i = divmod(t, 2)
+            nc.tensor.matmul_mx(
+                out=acc[:],
+                lhsT=codes[a, q][:, P * i : P * i + P].bitcast(E4M3),
+                lhsT_scale=planes[a, q][:, P * i : P * i + P],
+                rhs=rhs,
+                rhs_scale=rhs_scale,
+                start=False,
+                stop=(a == PASSES - 1),
+            )
+
+        groups = [(t, n0, HALF) for t in range(8) for n0 in (0, HALF)]
+        first, second = groups[:8], groups[8:15] + [(7, HALF + P * i, P) for i in range(4)]
+        acc = {}
+        result = {}
+
+        def open_group(g):
+            acc[g] = psum.tile([P, g[2]], F32, name="acc")
+
+        def drain(g):
+            t, n0, width = g
+            if n0 == 0:
+                result[t] = sb(f"out{t}", [P, N], F32)
+            cols = slice(n0, n0 + width)
+            nc.vector.tensor_tensor(out=result[t][:, cols], in0=acc[g][:], in1=bias[:, cols], op=ADD)
+            rows = slice(P * t, P * t + P)
+            if t == 7:
+                eng = nc.scalar if width == P and (n0 // P) % 2 == 0 else nc.sync
+                eng.dma_start(out=out[rows, cols], in_=result[t][:, cols])
+            elif n0 == HALF:
+                nc.sync.dma_start(out=out[rows, :], in_=result[t][:])
+
+        nc.scalar.copy(out=warm[:, 1:2], in_=warm[:, 0:1])
+
+        for g in first:
+            open_group(g)
+        for a in range(PASSES):
+            for n0 in (0, HALF):
+                for g in first:
+                    if g[1] == n0:
+                        x4_pass(acc[g], *g, a)
+
+        by = sb("by", [P, 32], F32)
+        nc.vector.transpose(out=by[:], in_=bz[:])
+        bx = sb("bx", [P, N], F32)
+        nc.vector.tensor_copy(
+            out=bx[:].rearrange("p (j r) -> p j r", r=32), in_=by[:].unsqueeze(2).to_broadcast([P, 32, 32])
+        )
+        cast(nc.vector.tensor_copy, 0, 0)
+        cast(nc.scalar.copy, 0, 1)
+        bias = sb("bias", [P, N], F32)
+        nc.vector.transpose(out=bias[:], in_=bx[:])
+        quant(0, 0)
+        cast(nc.vector.tensor_copy, 1, 0)
+        quant(0, 1)
+        quant(1, 0)
+        cast(nc.scalar.copy, 1, 1)
+        cast(nc.scalar.copy, 0, 2)
+        cast(nc.scalar.copy, 0, 3)
+        cast(nc.scalar.copy, 1, 3)
+
+        def finish(g):
+            for a in range(PASSES):
+                xr_pass(acc[g], *g, a)
+            drain(g)
+
+        after = {0: [(1, 1)], 4: [(0, 2)], 6: [(0, 3)]}
+        for i, g in enumerate(first):
+            finish(g)
+            for key in after.get(i, []):
+                quant(*key)
+        cast(nc.vector.tensor_copy, 1, 2)
+        quant(1, 3)
+        quant(1, 2)
+
+        LEAD = 3
+        for i in range(len(second) + LEAD):
+            if i < len(second):
+                open_group(second[i])
+                for a in range(PASSES):
+                    x4_pass(acc[second[i]], *second[i], a)
+            if i >= LEAD:
+                finish(second[i - LEAD])

@@ -15,7 +15,6 @@ P = 128
 K, N, T = 1024, 1024, 1024
 PASSES = K // 512
 HALF = 512
-Q = 256
 FLOPS = 2 * 2 * K * N * T
 
 
@@ -35,9 +34,9 @@ def tile_mix_xres_tm_bias_kernel(tc, x4_words, x4_scales, xr, w4_words, w4_scale
         x_half = [sb(f"x{h}", [P, PASSES * T], U8) for h in range(2)]
 
         nc.vector.memset(ws[:].bitcast(I32), 0)
-        nc.vector.memset(xs[:].bitcast(I32), 0)
         warm = sb("warm", [P, 2], F32)
         nc.vector.memset(warm[:, 0:1], 0.0)
+        nc.vector.memset(xs[:].bitcast(I32), 0)
 
         def load_scales(eng, plane, scales, quad):
             eng.dma_start(
@@ -45,97 +44,95 @@ def tile_mix_xres_tm_bias_kernel(tc, x4_words, x4_scales, xr, w4_words, w4_scale
                 in_=scales.bitcast(I32)[:, 4 * quad : 4 * quad + 4, :].rearrange("a r n -> r a n"),
             )
 
-        def load_x4(eng, h):
-            eng.dma_start(
+        def load_x4(h):
+            nc.sync.dma_start(
                 out=x_half[h][:].bitcast(I32).rearrange("p (a t) -> p a t", a=PASSES),
                 in_=x4_words.bitcast(I32)[:, :, 256 * h : 256 * h + 256].rearrange("a p t -> p a t"),
             )
 
-        nc.sync.dma_start(out=w[0][:].bitcast(I32), in_=w4_words[0].bitcast(I32))
-        load_x4(nc.scalar, 0)
-        for quad in range(4):
-            load_scales(nc.sync, ws, w4_scales, quad)
-            load_scales(nc.scalar, xs, x4_scales, quad)
+        def load_w4(eng, a):
+            eng.dma_start(out=w[a][:].bitcast(I32), in_=w4_words[a].bitcast(I32))
 
         xr_v = xr.rearrange("(a p j) t -> a p j t", a=PASSES, j=4)
+        raw_of = {}
+        grouped = {}
+        codes = {}
+        planes = {}
+        piece_of = {}
 
-        def load_xr(name, a, t0, width):
-            raw = sb(name, [P, 4, width], F32)
-            nc.sync.dma_start(out=raw[:], in_=xr_v[a, :, :, t0 : t0 + width])
-            return raw
+        def load_xr(a, *pieces):
+            first_tile = pieces[0][0]
+            width = P * sum(tiles for _, tiles in pieces)
+            raw = sb(f"raw{a}{first_tile}", [P, 4, width], F32)
+            nc.sync.dma_start(out=raw[:], in_=xr_v[a, :, :, P * first_tile : P * first_tile + width])
+            for t0, tiles in pieces:
+                key = (a, t0)
+                c0 = P * (t0 - first_tile)
+                cols = P * tiles
+                raw_of[key] = raw[:, :, c0 : c0 + cols]
+                grouped[key] = sb(f"g{a}{t0}", [P, cols * 4], BF16)
+                codes[key] = sb(f"c{a}{t0}", [P, cols], U32)
+                planes[key] = sb(f"s{a}{t0}", [P, cols], U8)
+                for i in range(tiles):
+                    piece_of[a, t0 + i] = (key, i)
 
-        raw00 = load_xr("raw00", 0, 0, 512)
-        nc.sync.dma_start(out=w[1][:].bitcast(I32), in_=w4_words[1].bitcast(I32))
+        load_xr(0, (0, 1))
+        load_scales(nc.sync, ws, w4_scales, 0)
+        load_scales(nc.sync, ws, w4_scales, 1)
+        load_scales(nc.scalar, ws, w4_scales, 2)
+        load_scales(nc.scalar, ws, w4_scales, 3)
+        load_w4(nc.scalar, 0)
+        load_xr(0, (1, 1))
+        load_x4(0)
+        for quad in range(4):
+            load_scales(nc.scalar, xs, x4_scales, quad)
+        load_w4(nc.sync, 1)
+        load_xr(1, (0, 2))
         bz = sb("bz", [P, 32], F32)
         for quad in range(4):
             nc.sync.dma_start(out=bz[32 * quad : 32 * quad + 32, :], in_=b.rearrange("(j q) -> j q", q=32))
-        raw10 = load_xr("raw10", 1, 0, 256)
-        raw11 = load_xr("raw11", 1, 256, 256)
-        load_x4(nc.sync, 1)
-        raw02 = load_xr("raw02", 0, 512, 512)
-        raw12 = load_xr("raw12", 1, 512, 512)
-        raw_of = {
-            (0, 0): raw00[:, :, 0:256],
-            (0, 1): raw00[:, :, 256:512],
-            (1, 0): raw10[:],
-            (1, 1): raw11[:],
-            (0, 2): raw02[:, :, 0:256],
-            (0, 3): raw02[:, :, 256:512],
-            (1, 2): raw12[:, :, 0:256],
-            (1, 3): raw12[:, :, 256:512],
-        }
-        grouped = {key: sb(f"g{key[0]}{key[1]}", [P, Q * 4], BF16) for key in raw_of}
-        codes = {key: sb(f"c{key[0]}{key[1]}", [P, Q], U32) for key in raw_of}
-        planes = {key: sb(f"s{key[0]}{key[1]}", [P, Q], U8) for key in raw_of}
+        load_xr(0, (2, 2))
+        load_xr(1, (2, 2))
+        load_x4(1)
+        load_xr(0, (4, 2), (6, 2))
+        load_xr(1, (4, 2), (6, 2))
 
-        def cast(eng_copy, a, q):
+        def cast(eng_copy, a, t0):
             eng_copy(
-                out=grouped[a, q][:].rearrange("p (c i j) -> p c j i", i=4, j=4),
-                in_=raw_of[a, q].rearrange("p j (c i) -> p c j i", i=4),
+                out=grouped[a, t0][:].rearrange("p (c i j) -> p c j i", i=4, j=4),
+                in_=raw_of[a, t0].rearrange("p j (c i) -> p c j i", i=4),
             )
 
-        def quant(a, q):
-            nc.vector.quantize_mx(out=codes[a, q][:].bitcast(E4M3), scales=planes[a, q][:], in_=grouped[a, q][:])
+        def quant(a, t0):
+            nc.vector.quantize_mx(out=codes[a, t0][:].bitcast(E4M3), scales=planes[a, t0][:], in_=grouped[a, t0][:])
 
-        def w_ops(a, n0, width):
-            return (
-                w[a][:, 2 * n0 : 2 * n0 + 2 * width].bitcast(E2M1),
-                ws[:, N * a + n0 : N * a + n0 + width],
-            )
-
-        def x4_pass(acc, t, n0, width, a):
-            rhs, rhs_scale = w_ops(a, n0, width)
-            h, i = divmod(t, 4)
-            nc.tensor.matmul_mx(
-                out=acc[:],
-                lhsT=x_half[h][:, 1024 * a + 256 * i : 1024 * a + 256 * i + 256].bitcast(E2M1),
-                lhsT_scale=xs[:, T * a + P * t : T * a + P * t + P],
-                rhs=rhs,
-                rhs_scale=rhs_scale,
-                start=(a == 0),
-                stop=False,
-            )
-
-        def xr_pass(acc, t, n0, width, a):
-            rhs, rhs_scale = w_ops(a, n0, width)
-            q, i = divmod(t, 2)
-            nc.tensor.matmul_mx(
-                out=acc[:],
-                lhsT=codes[a, q][:, P * i : P * i + P].bitcast(E4M3),
-                lhsT_scale=planes[a, q][:, P * i : P * i + P],
-                rhs=rhs,
-                rhs_scale=rhs_scale,
-                start=False,
-                stop=(a == PASSES - 1),
-            )
-
-        groups = [(t, n0, HALF) for t in range(8) for n0 in (0, HALF)]
-        first, second = groups[:8], groups[8:15] + [(7, HALF + P * i, P) for i in range(4)]
         acc = {}
+        passes_done = {}
         result = {}
 
-        def open_group(g):
-            acc[g] = psum.tile([P, g[2]], F32, name="acc")
+        def matmul(g, kind, a):
+            t, n0, width = g
+            if g not in acc:
+                acc[g] = psum.tile([P, width], F32, name="acc")
+                passes_done[g] = 0
+            if kind == "x4":
+                h, i = divmod(t, 4)
+                lhs = x_half[h][:, 1024 * a + 256 * i : 1024 * a + 256 * i + 256].bitcast(E2M1)
+                lhs_scale = xs[:, T * a + P * t : T * a + P * t + P]
+            else:
+                key, i = piece_of[a, t]
+                lhs = codes[key][:, P * i : P * i + P].bitcast(E4M3)
+                lhs_scale = planes[key][:, P * i : P * i + P]
+            nc.tensor.matmul_mx(
+                out=acc[g][:],
+                lhsT=lhs,
+                lhsT_scale=lhs_scale,
+                rhs=w[a][:, 2 * n0 : 2 * n0 + 2 * width].bitcast(E2M1),
+                rhs_scale=ws[:, N * a + n0 : N * a + n0 + width],
+                start=(passes_done[g] == 0),
+                stop=(passes_done[g] == 2 * PASSES - 1),
+            )
+            passes_done[g] += 1
 
         def drain(g):
             t, n0, width = g
@@ -150,54 +147,63 @@ def tile_mix_xres_tm_bias_kernel(tc, x4_words, x4_scales, xr, w4_words, w4_scale
             elif n0 == HALF:
                 nc.sync.dma_start(out=out[rows, :], in_=result[t][:])
 
+        groups = [(t, n0, HALF) for t in range(8) for n0 in (0, HALF)]
+        first, second = groups[:8], groups[8:15] + [(7, HALF + P * i, P) for i in range(4)]
+
         nc.scalar.copy(out=warm[:, 1:2], in_=warm[:, 0:1])
 
-        for g in first:
-            open_group(g)
-        for a in range(PASSES):
-            for n0 in (0, HALF):
-                for g in first:
-                    if g[1] == n0:
-                        x4_pass(acc[g], *g, a)
+        cast(nc.vector.tensor_copy, 0, 0)
+        quant(0, 0)
+        cast(nc.vector.tensor_copy, 0, 1)
+        quant(0, 1)
+        for g in first[0:4]:
+            matmul(g, "xr", 0)
+        for n0 in (0, HALF):
+            for g in first:
+                if g[1] == n0:
+                    matmul(g, "x4", 0)
+        for g in first[0:4]:
+            matmul(g, "x4", 1)
 
+        cast(nc.vector.tensor_copy, 1, 0)
         by = sb("by", [P, 32], F32)
         nc.vector.transpose(out=by[:], in_=bz[:])
+        quant(1, 0)
         bx = sb("bx", [P, N], F32)
         nc.vector.tensor_copy(
             out=bx[:].rearrange("p (j r) -> p j r", r=32), in_=by[:].unsqueeze(2).to_broadcast([P, 32, 32])
         )
-        cast(nc.vector.tensor_copy, 0, 0)
-        cast(nc.scalar.copy, 0, 1)
         bias = sb("bias", [P, N], F32)
         nc.vector.transpose(out=bias[:], in_=bx[:])
-        quant(0, 0)
-        cast(nc.vector.tensor_copy, 1, 0)
-        quant(0, 1)
-        quant(1, 0)
-        cast(nc.scalar.copy, 1, 1)
-        cast(nc.scalar.copy, 0, 2)
-        cast(nc.scalar.copy, 0, 3)
-        cast(nc.scalar.copy, 1, 3)
+        for key in ((0, 2), (1, 2), (0, 4), (0, 6), (1, 6)):
+            cast(nc.scalar.copy, *key)
 
-        def finish(g):
-            for a in range(PASSES):
-                xr_pass(acc[g], *g, a)
+        for g in first[0:4]:
+            matmul(g, "xr", 1)
             drain(g)
-
-        after = {0: [(1, 1)], 4: [(0, 2)], 6: [(0, 3)]}
-        for i, g in enumerate(first):
-            finish(g)
-            for key in after.get(i, []):
-                quant(*key)
-        cast(nc.vector.tensor_copy, 1, 2)
-        quant(1, 3)
+        quant(0, 2)
+        for g in first[4:8]:
+            matmul(g, "x4", 1)
+        for g in first[4:8]:
+            matmul(g, "xr", 0)
         quant(1, 2)
+        for i, g in enumerate(first[4:8]):
+            matmul(g, "xr", 1)
+            drain(g)
+            if i == 1:
+                quant(0, 4)
+        quant(0, 6)
+        cast(nc.vector.tensor_copy, 1, 4)
+        quant(1, 6)
+        quant(1, 4)
 
         LEAD = 3
         for i in range(len(second) + LEAD):
             if i < len(second):
-                open_group(second[i])
                 for a in range(PASSES):
-                    x4_pass(acc[second[i]], *second[i], a)
+                    matmul(second[i], "x4", a)
             if i >= LEAD:
-                finish(second[i - LEAD])
+                g = second[i - LEAD]
+                for a in range(PASSES):
+                    matmul(g, "xr", a)
+                drain(g)

@@ -31,7 +31,7 @@ def tile_mix_xres_tm_bias_kernel(tc, x4_words, x4_scales, xr, w4_words, w4_scale
         ws = sb("ws", [P, PASSES * N], U8)
         xs = sb("xs", [P, PASSES * T], U8)
         w = [sb(f"w{a}", [P, 2 * N], U8) for a in range(PASSES)]
-        x_half = [sb(f"x{h}", [P, PASSES * T], U8) for h in range(2)]
+        x = sb("x", [P, PASSES * 2 * T], U8)
 
         nc.vector.memset(ws[:].bitcast(I32), 0)
         warm = sb("warm", [P, 2], F32)
@@ -44,14 +44,14 @@ def tile_mix_xres_tm_bias_kernel(tc, x4_words, x4_scales, xr, w4_words, w4_scale
                 in_=scales.bitcast(I32)[:, 4 * quad : 4 * quad + 4, :].rearrange("a r n -> r a n"),
             )
 
-        def load_x4(h):
+        def load_x4():
             nc.sync.dma_start(
-                out=x_half[h][:].bitcast(I32).rearrange("p (a t) -> p a t", a=PASSES),
-                in_=x4_words.bitcast(I32)[:, :, 256 * h : 256 * h + 256].rearrange("a p t -> p a t"),
+                out=x[:].bitcast(I32).rearrange("p (a t) -> p a t", a=PASSES),
+                in_=x4_words.bitcast(I32).rearrange("a p t -> p a t"),
             )
 
-        def load_w4(eng, a):
-            eng.dma_start(out=w[a][:].bitcast(I32), in_=w4_words[a].bitcast(I32))
+        def load_w4(a):
+            nc.sync.dma_start(out=w[a][:].bitcast(I32), in_=w4_words[a].bitcast(I32))
 
         xr_v = xr.rearrange("(a p j) t -> a p j t", a=PASSES, j=4)
         raw_of = {}
@@ -77,23 +77,23 @@ def tile_mix_xres_tm_bias_kernel(tc, x4_words, x4_scales, xr, w4_words, w4_scale
                     piece_of[a, t0 + i] = (key, i)
 
         load_xr(0, (0, 1))
+        load_w4(0)
         load_scales(nc.sync, ws, w4_scales, 0)
         load_scales(nc.sync, ws, w4_scales, 1)
         load_scales(nc.scalar, ws, w4_scales, 2)
         load_scales(nc.scalar, ws, w4_scales, 3)
-        load_w4(nc.scalar, 0)
+        nc.scalar.copy(out=warm[:, 1:2], in_=warm[:, 0:1])
         load_xr(0, (1, 1))
-        load_x4(0)
+        load_xr(0, (2, 1), (3, 1))
+        load_x4()
         for quad in range(4):
             load_scales(nc.scalar, xs, x4_scales, quad)
-        load_w4(nc.sync, 1)
+        load_w4(1)
         load_xr(1, (0, 2))
         bz = sb("bz", [P, 32], F32)
         for quad in range(4):
             nc.sync.dma_start(out=bz[32 * quad : 32 * quad + 32, :], in_=b.rearrange("(j q) -> j q", q=32))
-        load_xr(0, (2, 2))
         load_xr(1, (2, 2))
-        load_x4(1)
         load_xr(0, (4, 2), (6, 2))
         load_xr(1, (4, 2), (6, 2))
 
@@ -116,8 +116,7 @@ def tile_mix_xres_tm_bias_kernel(tc, x4_words, x4_scales, xr, w4_words, w4_scale
                 acc[g] = psum.tile([P, width], F32, name="acc")
                 passes_done[g] = 0
             if kind == "x4":
-                h, i = divmod(t, 4)
-                lhs = x_half[h][:, 1024 * a + 256 * i : 1024 * a + 256 * i + 256].bitcast(E2M1)
+                lhs = x[:, 2 * (T * a + P * t) : 2 * (T * a + P * t + P)].bitcast(E2M1)
                 lhs_scale = xs[:, T * a + P * t : T * a + P * t + P]
             else:
                 key, i = piece_of[a, t]
@@ -141,7 +140,7 @@ def tile_mix_xres_tm_bias_kernel(tc, x4_words, x4_scales, xr, w4_words, w4_scale
             cols = slice(n0, n0 + width)
             nc.vector.tensor_tensor(out=result[t][:, cols], in0=acc[g][:], in1=bias[:, cols], op=ADD)
             rows = slice(P * t, P * t + P)
-            if t == 7:
+            if t >= 4:
                 eng = nc.scalar if width == P and (n0 // P) % 2 == 0 else nc.sync
                 eng.dma_start(out=out[rows, cols], in_=result[t][:, cols])
             elif n0 == HALF:
@@ -150,52 +149,50 @@ def tile_mix_xres_tm_bias_kernel(tc, x4_words, x4_scales, xr, w4_words, w4_scale
         groups = [(t, n0, HALF) for t in range(8) for n0 in (0, HALF)]
         first, second = groups[:8], groups[8:15] + [(7, HALF + P * i, P) for i in range(4)]
 
-        nc.scalar.copy(out=warm[:, 1:2], in_=warm[:, 0:1])
-
         cast(nc.vector.tensor_copy, 0, 0)
         quant(0, 0)
         cast(nc.vector.tensor_copy, 0, 1)
         quant(0, 1)
-        for g in first[0:4]:
+        cast(nc.vector.tensor_copy, 0, 2)
+        cast(nc.scalar.copy, 0, 3)
+        quant(0, 2)
+        quant(0, 3)
+        for g in first:
             matmul(g, "xr", 0)
-        for n0 in (0, HALF):
-            for g in first:
-                if g[1] == n0:
-                    matmul(g, "x4", 0)
+        for g in first:
+            matmul(g, "x4", 0)
         for g in first[0:4]:
             matmul(g, "x4", 1)
 
         cast(nc.vector.tensor_copy, 1, 0)
         by = sb("by", [P, 32], F32)
         nc.vector.transpose(out=by[:], in_=bz[:])
-        quant(1, 0)
         bx = sb("bx", [P, N], F32)
-        nc.vector.tensor_copy(
+        nc.scalar.copy(
             out=bx[:].rearrange("p (j r) -> p j r", r=32), in_=by[:].unsqueeze(2).to_broadcast([P, 32, 32])
         )
+        quant(1, 0)
         bias = sb("bias", [P, N], F32)
         nc.vector.transpose(out=bias[:], in_=bx[:])
-        for key in ((0, 2), (1, 2), (0, 4), (0, 6), (1, 6)):
+        for key in ((1, 2), (0, 4), (1, 4), (0, 6), (1, 6)):
             cast(nc.scalar.copy, *key)
 
-        for g in first[0:4]:
+        for i, g in enumerate(first[0:4]):
             matmul(g, "xr", 1)
             drain(g)
-        quant(0, 2)
+            if i == 0:
+                quant(1, 2)
         for g in first[4:8]:
             matmul(g, "x4", 1)
-        for g in first[4:8]:
-            matmul(g, "xr", 0)
-        quant(1, 2)
         for i, g in enumerate(first[4:8]):
             matmul(g, "xr", 1)
             drain(g)
-            if i == 1:
+            if i == 0:
                 quant(0, 4)
+            if i == 2:
+                quant(1, 4)
         quant(0, 6)
-        cast(nc.vector.tensor_copy, 1, 4)
         quant(1, 6)
-        quant(1, 4)
 
         LEAD = 3
         for i in range(len(second) + LEAD):

@@ -149,6 +149,12 @@ def tile_mix_xres_tm_bias_kernel(tc, x4_words, x4_scales, xr, w4_words, w4_scale
         groups = [(t, n0, HALF) for t in range(8) for n0 in (0, HALF)]
         first, second = groups[:8], groups[8:15] + [(7, HALF + P * i, P) for i in range(4)]
 
+        second_order = []
+        ahead = [second[0:5], second[5:6], second[6:7]] + [[g] for g in second[7:]]
+        follow = [second[0:1], second[1:3], second[3:7]] + [[g] for g in second[7:]]
+        for xs_groups, xr_groups in zip(ahead, follow):
+            second_order += [(g, "x4") for g in xs_groups] + [(g, "xr") for g in xr_groups]
+
         cast(nc.vector.tensor_copy, 0, 0)
         quant(0, 0)
         cast(nc.vector.tensor_copy, 0, 1)
@@ -194,13 +200,9 @@ def tile_mix_xres_tm_bias_kernel(tc, x4_words, x4_scales, xr, w4_words, w4_scale
         quant(0, 6)
         quant(1, 6)
 
-        LEAD = 3
-        for i in range(len(second) + LEAD):
-            if i < len(second):
-                for a in range(PASSES):
-                    matmul(second[i], "x4", a)
-            if i >= LEAD:
-                g = second[i - LEAD]
-                for a in range(PASSES):
-                    matmul(g, "xr", a)
+        for step in second_order:
+            g, kind = step
+            for a in range(PASSES):
+                matmul(g, kind, a)
+            if kind == "xr":
                 drain(g)

from contextlib import ExitStack

import concourse.mybir as mybir

F32 = mybir.dt.float32
BF16 = mybir.dt.bfloat16
I32 = mybir.dt.int32
U32 = mybir.dt.uint32
U8 = mybir.dt.uint8
E4M3 = mybir.dt.float8_e4m3fn_x4
E2M1 = mybir.dt.float4_e2m1fn_x4
ADD = mybir.AluOpType.add

P = 128
K, N, T = 1024, 1024, 1024
PASSES = K // 512
HALF = 512
FLOPS = 2 * 2 * K * N * T


def tile_mix_xres_tm_bias_kernel(tc, x4_words, x4_scales, xr, w4_words, w4_scales, b, out):
    nc = tc.nc
    with ExitStack() as ctx:
        keep = ctx.enter_context(tc.tile_pool(name="keep", bufs=1))
        psum = ctx.enter_context(tc.psum_pool(name="psum", bufs=8))
        ctx.enter_context(tc.manual_schedule())

        def sb(name, shape, dtype):
            return keep.tile(shape, dtype, name=name, align_bytes=256)

        ws = sb("ws", [P, PASSES * N], U8)
        xs = sb("xs", [P, PASSES * T], U8)
        w = [sb(f"w{a}", [P, 2 * N], U8) for a in range(PASSES)]
        x = sb("x", [P, PASSES * 2 * T], U8)

        nc.vector.memset(ws[:].bitcast(I32), 0)
        warm = sb("warm", [P, 2], F32)
        nc.vector.memset(warm[:, 0:1], 0.0)
        nc.vector.memset(xs[:].bitcast(I32), 0)

        def load_scales(eng, plane, scales, quad):
            eng.dma_start(
                out=plane[32 * quad : 32 * quad + 4, :].bitcast(I32).rearrange("p (a n) -> p a n", a=PASSES),
                in_=scales.bitcast(I32)[:, 4 * quad : 4 * quad + 4, :].rearrange("a r n -> r a n"),
            )

        def load_x4():
            nc.sync.dma_start(
                out=x[:].bitcast(I32).rearrange("p (a t) -> p a t", a=PASSES),
                in_=x4_words.bitcast(I32).rearrange("a p t -> p a t"),
            )

        def load_w4(a):
            nc.sync.dma_start(out=w[a][:].bitcast(I32), in_=w4_words[a].bitcast(I32))

        xr_v = xr.rearrange("(a p j) t -> a p j t", a=PASSES, j=4)
        raw_of = {}
        grouped = {}
        codes = {}
        planes = {}
        piece_of = {}

        def load_xr(a, *pieces):
            first_tile = pieces[0][0]
            width = P * sum(tiles for _, tiles in pieces)
            raw = sb(f"raw{a}{first_tile}", [P, 4, width], F32)
            nc.sync.dma_start(out=raw[:], in_=xr_v[a, :, :, P * first_tile : P * first_tile + width])
            for t0, tiles in pieces:
                key = (a, t0)
                c0 = P * (t0 - first_tile)
                cols = P * tiles
                raw_of[key] = raw[:, :, c0 : c0 + cols]
                grouped[key] = sb(f"g{a}{t0}", [P, cols * 4], BF16)
                codes[key] = sb(f"c{a}{t0}", [P, cols], U32)
                planes[key] = sb(f"s{a}{t0}", [P, cols], U8)
                for i in range(tiles):
                    piece_of[a, t0 + i] = (key, i)

        load_xr(0, (0, 1))
        load_w4(0)
        load_scales(nc.sync, ws, w4_scales, 0)
        load_scales(nc.sync, ws, w4_scales, 1)
        load_scales(nc.scalar, ws, w4_scales, 2)
        load_scales(nc.scalar, ws, w4_scales, 3)
        nc.scalar.copy(out=warm[:, 1:2], in_=warm[:, 0:1])
        load_xr(0, (1, 1))
        load_xr(0, (2, 1), (3, 1))
        load_x4()
        for quad in range(4):
            load_scales(nc.scalar, xs, x4_scales, quad)
        load_w4(1)
        load_xr(1, (0, 2))
        bz = sb("bz", [P, 32], F32)
        for quad in range(4):
            nc.sync.dma_start(out=bz[32 * quad : 32 * quad + 32, :], in_=b.rearrange("(j q) -> j q", q=32))
        load_xr(1, (2, 2))
        load_xr(0, (4, 2), (6, 2))
        load_xr(1, (4, 2), (6, 2))

        def cast(eng_copy, a, t0):
            eng_copy(
                out=grouped[a, t0][:].rearrange("p (c i j) -> p c j i", i=4, j=4),
                in_=raw_of[a, t0].rearrange("p j (c i) -> p c j i", i=4),
            )

        def quant(a, t0):
            nc.vector.quantize_mx(out=codes[a, t0][:].bitcast(E4M3), scales=planes[a, t0][:], in_=grouped[a, t0][:])

        acc = {}
        passes_done = {}
        result = {}

        def matmul(g, kind, a):
            t, n0, width = g
            if g not in acc:
                acc[g] = psum.tile([P, width], F32, name="acc")
                passes_done[g] = 0
            if kind == "x4":
                lhs = x[:, 2 * (T * a + P * t) : 2 * (T * a + P * t + P)].bitcast(E2M1)
                lhs_scale = xs[:, T * a + P * t : T * a + P * t + P]
            else:
                key, i = piece_of[a, t]
                lhs = codes[key][:, P * i : P * i + P].bitcast(E4M3)
                lhs_scale = planes[key][:, P * i : P * i + P]
            nc.tensor.matmul_mx(
                out=acc[g][:],
                lhsT=lhs,
                lhsT_scale=lhs_scale,
                rhs=w[a][:, 2 * n0 : 2 * n0 + 2 * width].bitcast(E2M1),
                rhs_scale=ws[:, N * a + n0 : N * a + n0 + width],
                start=(passes_done[g] == 0),
                stop=(passes_done[g] == 2 * PASSES - 1),
            )
            passes_done[g] += 1

        def drain(g):
            t, n0, width = g
            if n0 == 0:
                result[t] = sb(f"out{t}", [P, N], F32)
            cols = slice(n0, n0 + width)
            nc.vector.tensor_tensor(out=result[t][:, cols], in0=acc[g][:], in1=bias[:, cols], op=ADD)
            rows = slice(P * t, P * t + P)
            if t >= 4:
                eng = nc.scalar if width == P and (n0 // P) % 2 == 0 else nc.sync
                eng.dma_start(out=out[rows, cols], in_=result[t][:, cols])
            elif n0 == HALF:
                nc.sync.dma_start(out=out[rows, :], in_=result[t][:])

        groups = [(t, n0, HALF) for t in range(8) for n0 in (0, HALF)]
        first, second = groups[:8], groups[8:15] + [(7, HALF + P * i, P) for i in range(4)]

        second_order = []
        ahead = [second[0:5], second[5:6], second[6:7]] + [[g] for g in second[7:]]
        follow = [second[0:1], second[1:3], second[3:7]] + [[g] for g in second[7:]]
        for xs_groups, xr_groups in zip(ahead, follow):
            second_order += [(g, "x4") for g in xs_groups] + [(g, "xr") for g in xr_groups]

        cast(nc.vector.tensor_copy, 0, 0)
        quant(0, 0)
        cast(nc.vector.tensor_copy, 0, 1)
        quant(0, 1)
        cast(nc.vector.tensor_copy, 0, 2)
        cast(nc.scalar.copy, 0, 3)
        quant(0, 2)
        quant(0, 3)
        for g in first:
            matmul(g, "xr", 0)
        for g in first:
            matmul(g, "x4", 0)
        for g in first[0:4]:
            matmul(g, "x4", 1)

        cast(nc.vector.tensor_copy, 1, 0)
        by = sb("by", [P, 32], F32)
        nc.vector.transpose(out=by[:], in_=bz[:])
        bx = sb("bx", [P, N], F32)
        nc.scalar.copy(
            out=bx[:].rearrange("p (j r) -> p j r", r=32), in_=by[:].unsqueeze(2).to_broadcast([P, 32, 32])
        )
        quant(1, 0)
        bias = sb("bias", [P, N], F32)
        nc.vector.transpose(out=bias[:], in_=bx[:])
        for key in ((1, 2), (0, 4), (1, 4), (0, 6), (1, 6)):
            cast(nc.scalar.copy, *key)

        for i, g in enumerate(first[0:4]):
            matmul(g, "xr", 1)
            drain(g)
            if i == 0:
                quant(1, 2)
        for g in first[4:8]:
            matmul(g, "x4", 1)
        for i, g in enumerate(first[4:8]):
            matmul(g, "xr", 1)
            drain(g)
            if i == 0:
                quant(0, 4)
            if i == 2:
                quant(1, 4)
        quant(0, 6)
        quant(1, 6)

        for step in second_order:
            g, kind = step
            for a in range(PASSES):
                matmul(g, kind, a)
            if kind == "xr":
                drain(g)
